import numpy as np
import ml_dtypes


def mxq(x, axis, fmt="e4m3"):
    dtype, down = {"e4m3": (ml_dtypes.float8_e4m3fn, 7), "e5m2": (ml_dtypes.float8_e5m2, 14)}[fmt]
    v = np.moveaxis(np.asarray(x, np.float32).astype(ml_dtypes.bfloat16).astype(np.float64), axis, -1)
    blocks = v.reshape(v.shape[:-1] + (-1, 32))
    amax = np.abs(blocks).max(-1, keepdims=True)
    byte = np.maximum(np.where(amax > 0, np.frexp(amax)[1] - 1 + 127, 0) - down, 1)
    scale = np.exp2(byte - 127.0)
    codes = (blocks / scale).astype(np.float32).astype(dtype).astype(np.float64)
    return np.moveaxis((codes * scale).reshape(v.shape), -1, axis)


WIDE = False


def mx_kscale(k):
    if not WIDE:
        return np.ones(k)
    levels = np.array([30, -30])
    if k % 512:
        return np.exp2(np.random.permutation(np.resize(levels, k // 32))).repeat(32)
    a = np.empty((k // 512, 16))
    for p in range(k // 512):
        a[p, :8] = np.random.permutation(np.resize(levels, 8))
        for g in range(8):
            far = levels[np.abs(levels - a[p, g]) >= 10]
            a[p, g + 8] = far[np.random.randint(len(far))]
    return np.exp2(a.ravel()).repeat(32)


BF16 = ml_dtypes.bfloat16


def bf(x):
    return np.asarray(x, np.float32).astype(BF16)


def f64(x):
    return np.asarray(x).astype(np.float64)


E2M1 = np.array([0.0, 0.5, 1.0, 1.5, 2.0, 3.0, 4.0, 6.0, -0.0, -0.5, -1.0, -1.5, -2.0, -3.0, -4.0, -6.0])


def pack_weight(w, fmt):
    k, n = w.shape
    w = f64(bf(w)).reshape(k // 32, 32, n)
    amax = np.abs(w).max(1)
    if fmt == "e4m3":
        byte = np.frexp(amax)[1] - 1 + 127 - 7
    else:
        mant, ex = np.frexp(amax / 6.0)
        byte = np.where(mant > 0.5, ex, ex - 1) + 127
    byte = np.clip(np.where(amax > 0, byte, 1), 1, 254)
    scaled = (w * np.exp2(127.0 - byte)[:, None, :]).reshape(k, n).astype(np.float32)
    by_word = np.ascontiguousarray(scaled.reshape(k // 512, 128, 4, n).transpose(0, 1, 3, 2))
    if fmt == "e4m3":
        words = by_word.astype(ml_dtypes.float8_e4m3fn).view(np.uint8)
    else:
        c = by_word.astype(ml_dtypes.float4_e2m1fn).view(np.uint8) & 0xF
        words = c[..., 0::2] | (c[..., 1::2] << 4)
    return np.ascontiguousarray(words), np.ascontiguousarray(byte.astype(np.uint8).reshape(k // 512, 16, n))


def unpack_weight(words, scales, fmt):
    g, p, n, _ = words.shape
    if fmt == "e4m3":
        vals = np.ascontiguousarray(words).view(ml_dtypes.float8_e4m3fn).astype(np.float64)
    else:
        nib = np.empty((g, p, n, 4), np.uint8)
        nib[..., 0::2] = words & 0xF
        nib[..., 1::2] = words >> 4
        vals = E2M1[nib]
    vals = vals * np.repeat(np.exp2(scales.astype(np.float64) - 127.0), 8, axis=1)[..., None]
    return vals.transpose(0, 1, 3, 2).reshape(g * 512, n)
def pack4(w):
    words, scales = pack_weight(w, "e2m1")
    return words.reshape(words.shape[0], 128, -1), scales


def unpack4(words, scales):
    return unpack_weight(words.reshape(words.shape[0], 128, -1, 2), scales, "e2m1")


M, K, F, N = 512, 1024, 2048, 1024


def setup_inputs():
    s, t = mx_kscale(K), mx_kscale(F)
    obj = np.sqrt(K) * np.random.random((K, 1))
    det = np.sqrt(F) * np.random.random((1, F))
    foc = np.sqrt(F) * np.random.random((1, N))
    fwd = np.pi * (obj - det) ** 2
    back = np.pi * (det.T - foc) ** 2
    fs, bs = np.sqrt(2 / K) / s[:, None] * t, np.sqrt(2 / F) / t[:, None]
    cos_words, cos_scales = pack4(np.cos(fwd) * fs)
    sin_words, sin_scales = pack4(np.sin(fwd) * fs)
    return {"x": bf(np.random.standard_normal((M, K)) * s),
            "cos_words": cos_words, "cos_scales": cos_scales,
            "sin_words": sin_words, "sin_scales": sin_scales,
            "meas": bf(np.abs(1.2 + 0.5 * np.random.standard_normal((M, F))) * t),
            "back_cos": bf(np.cos(back) * bs),
            "back_sin": bf(-np.sin(back) * bs)}


def reference(x, cos_words, cos_scales, sin_words, sin_scales, meas, back_cos, back_sin):
    xq = mxq(f64(x), 1, "e4m3")
    re = xq @ unpack4(cos_words, cos_scales)
    im = xq @ unpack4(sin_words, sin_scales)
    e = np.sqrt(re * re + im * im) - f64(meas)
    eq = mxq(e, 1, "e5m2")
    out_re = eq @ mxq(f64(back_cos), 0, "e4m3")
    out_im = eq @ mxq(f64(back_sin), 0, "e4m3")
    return out_re, out_im

@@ -1,0 +1,249 @@
+from contextlib import ExitStack
+
+import concourse.mybir as mybir
+from concourse.masks import make_identity
+
+M, K, F, N = 512, 1024, 2048, 1024
+FLOPS = 2 * M * K * F * 2 + 2 * M * F * N * 2
+
+F32 = mybir.dt.float32
+BF16 = mybir.dt.bfloat16
+I32 = mybir.dt.int32
+U32 = mybir.dt.uint32
+U8 = mybir.dt.uint8
+E4M3 = mybir.dt.float8_e4m3fn_x4
+E5M2 = mybir.dt.float8_e5m2_x4
+E2M1 = mybir.dt.float4_e2m1fn_x4
+ACT = mybir.ActivationFunctionType
+ALU = mybir.AluOpType
+
+P = 128
+NB = 512
+
+
+def tile_fresnel_magnitude_residual_s9_kernel(
+    tc, x, cos_words, cos_scales, sin_words, sin_scales, meas, back_cos, back_sin, out_re, out_im
+):
+    nc = tc.nc
+    words = (cos_words, sin_words)
+    scales = (cos_scales, sin_scales)
+    back = (back_cos, back_sin)
+    outs = (out_re, out_im)
+
+    with ExitStack() as ctx:
+        keep = ctx.enter_context(tc.tile_pool(name="keep", bufs=1))
+        work = ctx.enter_context(tc.tile_pool(name="work", bufs=3))
+        ps = ctx.enter_context(tc.psum_pool(name="ps", bufs=2))
+
+        ident = keep.tile([P, P], F32, name="ident", align_bytes=64)
+        make_identity(nc, ident[:])
+        warm = keep.tile([P, 1], F32, name="warm")
+        nc.vector.memset(warm[:], 1.0)
+        nc.scalar.activation(out=warm[:], in_=warm[:], func=ACT.Sqrt)
+        planes = keep.tile([P, 2 * 2 * F], U8, name="planes", align_bytes=64)
+        nc.vector.memset(planes[:].bitcast(I32), 0)
+
+        x_sb = [keep.tile([P, K], BF16, name="x%d" % m, align_bytes=64) for m in range(4)]
+        meas_sb = [keep.tile([P, F], BF16, name="meas%d" % m, align_bytes=64) for m in range(4)]
+        fwd = [keep.tile([P, 2 * 2 * F], U8, name="fwd%d" % a, align_bytes=64) for a in range(2)]
+        raw = [[keep.tile([P, 4, N], BF16, name="raw%d%d" % (a, g), align_bytes=64) for g in range(4)] for a in range(2)]
+
+        def load_x(m):
+            nc.sync.dma_start(out=x_sb[m][:], in_=x[m * P : (m + 1) * P, :])
+
+        def load_meas(m):
+            nc.sync.dma_start(out=meas_sb[m][:], in_=meas[m * P : (m + 1) * P, :])
+
+        def load_scales():
+            for a in range(2):
+                for r in range(4):
+                    dst = planes[r:P:32, a * 2 * F : (a + 1) * 2 * F].bitcast(I32)
+                    src = scales[a][:, r:16:4, :].bitcast(I32)
+                    nc.sync.dma_start(out=dst.rearrange("q (g n) -> q g n", g=2), in_=src.rearrange("g q n -> q g n"))
+
+        def load_fwd(lo, hi):
+            for a in range(2):
+                dst = fwd[a][:].bitcast(I32).rearrange("p (g w) -> p g w", g=2)[:, :, lo // 2 : hi // 2]
+                src = words[a].bitcast(I32)[:, :, lo // 2 : hi // 2].rearrange("g p w -> p g w")
+                nc.sync.dma_start(out=dst, in_=src)
+
+        def load_back(a, g):
+            nc.sync.dma_start(out=raw[a][g][:], in_=back[a][g * 512 : (g + 1) * 512, :].rearrange("(p j) w -> p j w", j=4))
+
+        load_x(0)
+        load_scales()
+        load_fwd(0, 512)
+        load_back(0, 0)
+        load_fwd(512, 1024)
+        load_meas(0)
+        load_fwd(1024, 2048)
+        load_back(0, 1)
+        load_x(1)
+        load_back(0, 2)
+        load_meas(1)
+        load_back(0, 3)
+        load_x(2)
+        load_back(1, 0)
+        load_back(1, 1)
+        load_meas(2)
+        load_x(3)
+        load_back(1, 2)
+        load_back(1, 3)
+        load_meas(3)
+
+        xc = [keep.tile([P, 256], U32, name="xc%d" % m, align_bytes=64) for m in range(4)]
+        xs = [keep.tile([P, 256], U8, name="xs%d" % m, align_bytes=64) for m in range(4)]
+
+        def do_x(m):
+            xw = x_sb[m][:].bitcast(F32)
+            bank = ps.tile([P, 4, P], F32, name="tp", tag="tp", bufs=1)
+            for g in range(2):
+                for u in range(2):
+                    nc.tensor.transpose(bank[:, 2 * g + u, :], xw[:, 256 * g + u : 256 * (g + 1) : 2], ident[:])
+            grp = work.tile([P, 1024], BF16, name="xg", align_bytes=64, bufs=2)
+            nc.vector.tensor_copy(
+                out=grp[:].bitcast(F32).rearrange("p (g r u) -> p g r u", g=2, u=2),
+                in_=bank[:].rearrange("p (g u) r -> p g r u", u=2),
+            )
+            nc.vector.quantize_mx(out=xc[m][:].bitcast(E4M3), scales=xs[m][:], in_=grp[:])
+
+        bc = [[[keep.tile([P, NB], U32, name="bc%d%d%d" % (a, g, h), align_bytes=64) for h in range(2)] for g in range(4)] for a in range(2)]
+        bs = [[[keep.tile([P, NB], U8, name="bs%d%d%d" % (a, g, h), align_bytes=64) for h in range(2)] for g in range(4)] for a in range(2)]
+
+        def do_back(k, on_scalar):
+            a, g, h = (0, k // 2, k % 2) if k < 8 else (1, k % 4, (k - 8) // 4)
+            grp = work.tile([P, NB, 4], BF16, name="bg", align_bytes=64, bufs=4)
+            dst = grp[:].rearrange("p (c i) t -> p c t i", i=4)
+            src = raw[a][g][:, :, h * NB : (h + 1) * NB].rearrange("p t (c i) -> p c t i", i=4)
+            if on_scalar:
+                nc.scalar.copy(out=dst, in_=src)
+            else:
+                nc.vector.tensor_copy(out=dst, in_=src)
+            nc.vector.quantize_mx(
+                out=bc[a][g][h][:].bitcast(E4M3), scales=bs[a][g][h][:], in_=grp[:].rearrange("p c t -> p (c t)")
+            )
+
+        banks = {}
+
+        def stage1(u):
+            m, c = divmod(u, 4)
+            re = ps.tile([P, NB], F32, name="re", tag="re", bufs=2)
+            im = ps.tile([P, NB], F32, name="im", tag="im", bufs=2)
+            banks[u] = (re, im)
+            for g in range(2):
+                for a in range(2):
+                    col = g * F + c * NB
+                    nc.tensor.matmul_mx(
+                        out=banks[u][a][:],
+                        lhsT=xc[m][:, g * P : (g + 1) * P].bitcast(E4M3),
+                        lhsT_scale=xs[m][:, g * P : (g + 1) * P],
+                        rhs=fwd[a][:, 2 * col : 2 * (col + NB)].bitcast(E2M1),
+                        rhs_scale=planes[:, a * 2 * F + col : a * 2 * F + col + NB],
+                        start=(g == 0),
+                        stop=(g == 1),
+                    )
+
+        r2 = {}
+        e_sb = {}
+
+        def squares(u):
+            re, im = banks[u]
+            sr = work.tile([P, NB], F32, name="sr", align_bytes=64)
+            si = work.tile([P, NB], F32, name="si", align_bytes=64)
+            nc.scalar.activation(out=sr[:], in_=re[:], func=ACT.Square)
+            nc.scalar.activation(out=si[:], in_=im[:], func=ACT.Square)
+            r2[u] = work.tile([P, NB], F32, name="rr", align_bytes=64)
+            nc.vector.tensor_tensor(out=r2[u][:], in0=sr[:], in1=si[:], op=ALU.add)
+
+        def residual(u):
+            m, c = divmod(u, 4)
+            mag = work.tile([P, NB], F32, name="mag", align_bytes=64)
+            nc.scalar.activation(out=mag[:], in_=r2[u][:], func=ACT.Sqrt)
+            if u % 2 == 0:
+                e_sb[u // 2] = work.tile([P, 2 * NB], BF16, name="e", align_bytes=64)
+            lo = (u % 2) * NB
+            nc.vector.tensor_tensor(
+                out=e_sb[u // 2][:, lo : lo + NB].rearrange("m (u p e) -> m u p e", u=2, e=2),
+                in0=mag[:].rearrange("m (p u e) -> m u p e", u=2, e=2),
+                in1=meas_sb[m][:, c * NB : (c + 1) * NB].rearrange("m (p u e) -> m u p e", u=2, e=2),
+                op=ALU.subtract,
+            )
+
+        ec = [keep.tile([P, 256], U32, name="ec%d" % k, align_bytes=64) for k in range(8)]
+        es = [keep.tile([P, 256], U8, name="es%d" % k, align_bytes=64) for k in range(8)]
+        et = {}
+
+        def turn(k):
+            ew = e_sb[k][:].bitcast(F32)
+            et[k] = ps.tile([P, 4, P], F32, name="tp", tag="tp", bufs=1)
+            for q in range(4):
+                nc.tensor.transpose(et[k][:, q, :], ew[:, q * P : (q + 1) * P], ident[:])
+
+        def quant_e(k):
+            grp = work.tile([P, 1024], BF16, name="eg", align_bytes=64, bufs=2)
+            nc.scalar.copy(
+                out=grp[:].bitcast(F32).rearrange("p (c r u) -> p c r u", c=2, u=2),
+                in_=et[k][:].rearrange("p (c u) r -> p c r u", u=2),
+            )
+            nc.vector.quantize_mx(out=ec[k][:].bitcast(E5M2), scales=es[k][:], in_=grp[:])
+
+        acc = {}
+
+        def cell(m, a, h):
+            acc[m, a, h] = ps.tile([P, NB], F32, name="acc", tag="acc", bufs=3)
+            for g in range(4):
+                k, lo = 2 * m + g // 2, (g % 2) * P
+                nc.tensor.matmul_mx(
+                    out=acc[m, a, h][:],
+                    lhsT=ec[k][:, lo : lo + P].bitcast(E5M2),
+                    lhsT_scale=es[k][:, lo : lo + P],
+                    rhs=bc[a][g][h][:].bitcast(E4M3),
+                    rhs_scale=bs[a][g][h][:],
+                    start=(g == 0),
+                    stop=(g == 3),
+                )
+
+        def store(m, a, h, on_scalar):
+            res = work.tile([P, NB], F32, name="res", align_bytes=64, bufs=4)
+            if on_scalar:
+                nc.scalar.copy(out=res[:], in_=acc[m, a, h][:])
+            else:
+                nc.vector.tensor_copy(out=res[:], in_=acc[m, a, h][:])
+            nc.sync.dma_start(out=outs[a][m * P : (m + 1) * P, h * NB : (h + 1) * NB], in_=res[:])
+
+        e_slot = {}
+        b_slot = {}
+        pending = [(m, a, h) for a in range(2) for h in range(2) for m in range(4)]
+        n_out = 0
+        do_x(0)
+        stage1(0)
+        stage1(1)
+        for u in range(24):
+            if u < 16:
+                squares(u)
+            if u + 2 < 16:
+                stage1(u + 2)
+            if 1 <= u <= 16:
+                residual(u - 1)
+            if 2 <= u <= 16 and u % 2 == 0:
+                turn(u // 2 - 1)
+            if 3 <= u <= 17 and u % 2 == 1:
+                quant_e((u - 3) // 2)
+                e_slot[(u - 3) // 2] = u
+            if u in (1, 3, 5):
+                do_x((u + 1) // 2)
+            for k in range(16):
+                if (k * 3) // 4 == u:
+                    do_back(k, k in (1, 4, 7))
+                    b_slot[k] = u
+            ready = [
+                (m, a, h)
+                for m, a, h in pending
+                if all(e_slot.get(2 * m + i, 99) < u for i in range(2))
+                and all(b_slot.get(k, 99) < u for k in ((h, 2 + h, 4 + h, 6 + h) if a == 0 else range(8 + 4 * h, 12 + 4 * h)))
+            ]
+            for m, a, h in ready[:3]:
+                pending.remove((m, a, h))
+                cell(m, a, h)
+                store(m, a, h, n_out % 2 == 0)
+                n_out += 1

@@ -18,6 +18,9 @@ ACT = mybir.ActivationFunctionType
 ALU = mybir.AluOpType
 
 P = 128
+T_UNITS = (4, 5, 6, 7, 8, 9, 10, 11)
+FW = ((0, 512), (512, 1024), (1024, 2048))
+SPLIT = ((0, 0),)
 NB = 512
 
 
@@ -43,10 +46,15 @@ def tile_fresnel_magnitude_residual_s9_kernel(
         planes = keep.tile([P, 2 * 2 * F], U8, name="planes", align_bytes=64)
         nc.vector.memset(planes[:].bitcast(I32), 0)
 
+        ctx.enter_context(tc.manual_schedule())
         x_sb = [keep.tile([P, K], BF16, name="x%d" % m, align_bytes=64) for m in range(4)]
         meas_sb = [keep.tile([P, F], BF16, name="meas%d" % m, align_bytes=64) for m in range(4)]
-        fwd = [keep.tile([P, 2 * 2 * F], U8, name="fwd%d" % a, align_bytes=64) for a in range(2)]
-        raw = [[keep.tile([P, 4, N], BF16, name="raw%d%d" % (a, g), align_bytes=64) for g in range(4)] for a in range(2)]
+        fwd = [{c: keep.tile([P, 2, 2 * (hi - lo)], U8, name="fwd%d%d" % (a, c), align_bytes=64) for c, (lo, hi) in enumerate(FW)} for a in range(2)]
+        raw = {}
+        for a in range(2):
+            for g in range(4):
+                for h in range(2 if (a, g) in SPLIT else 1):
+                    raw[a, g, h] = keep.tile([P, 4, NB if (a, g) in SPLIT else N], BF16, name="raw%d%d%d" % (a, g, h), align_bytes=64)
 
         def load_x(m):
             nc.sync.dma_start(out=x_sb[m][:], in_=x[m * P : (m + 1) * P, :])
@@ -54,73 +62,93 @@ def tile_fresnel_magnitude_residual_s9_kernel(
         def load_meas(m):
             nc.sync.dma_start(out=meas_sb[m][:], in_=meas[m * P : (m + 1) * P, :])
 
-        def load_scales():
-            for a in range(2):
+        def load_scales(a, queue):
+            if True:
                 for r in range(4):
                     dst = planes[r:P:32, a * 2 * F : (a + 1) * 2 * F].bitcast(I32)
                     src = scales[a][:, r:16:4, :].bitcast(I32)
-                    nc.sync.dma_start(out=dst.rearrange("q (g n) -> q g n", g=2), in_=src.rearrange("g q n -> q g n"))
+                    queue.dma_start(out=dst.rearrange("q (g n) -> q g n", g=2), in_=src.rearrange("g q n -> q g n"))
 
-        def load_fwd(lo, hi):
+        def load_fwd(c):
+            lo, hi = FW[c]
             for a in range(2):
-                dst = fwd[a][:].bitcast(I32).rearrange("p (g w) -> p g w", g=2)[:, :, lo // 2 : hi // 2]
-                src = words[a].bitcast(I32)[:, :, lo // 2 : hi // 2].rearrange("g p w -> p g w")
-                nc.sync.dma_start(out=dst, in_=src)
+                nc.sync.dma_start(
+                    out=fwd[a][c][:].bitcast(I32),
+                    in_=words[a].bitcast(I32)[:, :, lo // 2 : hi // 2].rearrange("g p w -> p g w"),
+                )
 
-        def load_back(a, g):
-            nc.sync.dma_start(out=raw[a][g][:], in_=back[a][g * 512 : (g + 1) * 512, :].rearrange("(p j) w -> p j w", j=4))
+        def load_back(a, g, h=0):
+            src = back[a][g * 512 : (g + 1) * 512, :].rearrange("(p j) w -> p j w", j=4)
+            if (a, g) in SPLIT:
+                src = src[:, :, h * NB : (h + 1) * NB]
+            nc.sync.dma_start(out=raw[a, g, h][:], in_=src)
 
         load_x(0)
-        load_scales()
-        load_fwd(0, 512)
-        load_back(0, 0)
-        load_fwd(512, 1024)
-        load_meas(0)
-        load_fwd(1024, 2048)
-        load_back(0, 1)
+        load_fwd(0)
+        load_back(0, 0, 1)
+        load_scales(1, nc.sync)
+        load_back(0, 0, 0)
+        load_fwd(1)
+        load_scales(0, nc.sync)
+        load_fwd(2)
         load_x(1)
-        load_back(0, 2)
         load_meas(1)
-        load_back(0, 3)
         load_x(2)
-        load_back(1, 0)
+        load_meas(0)
+        load_back(0, 3)
         load_back(1, 1)
-        load_meas(2)
         load_x(3)
+        load_meas(2)
+        load_back(0, 2)
         load_back(1, 2)
-        load_back(1, 3)
+        load_back(0, 1)
         load_meas(3)
+        load_back(1, 0)
+        load_back(1, 3)
 
         xc = [keep.tile([P, 256], U32, name="xc%d" % m, align_bytes=64) for m in range(4)]
         xs = [keep.tile([P, 256], U8, name="xs%d" % m, align_bytes=64) for m in range(4)]
 
-        def do_x(m):
+        xg = {}
+
+        def turn_x(m):
             xw = x_sb[m][:].bitcast(F32)
             bank = ps.tile([P, 4, P], F32, name="tp", tag="tp", bufs=1)
             for g in range(2):
                 for u in range(2):
                     nc.tensor.transpose(bank[:, 2 * g + u, :], xw[:, 256 * g + u : 256 * (g + 1) : 2], ident[:])
-            grp = work.tile([P, 1024], BF16, name="xg", align_bytes=64, bufs=2)
+            xg[m] = work.tile([P, 1024], BF16, name="xg", align_bytes=64, bufs=2)
             nc.vector.tensor_copy(
-                out=grp[:].bitcast(F32).rearrange("p (g r u) -> p g r u", g=2, u=2),
+                out=xg[m][:].bitcast(F32).rearrange("p (g r u) -> p g r u", g=2, u=2),
                 in_=bank[:].rearrange("p (g u) r -> p g r u", u=2),
             )
-            nc.vector.quantize_mx(out=xc[m][:].bitcast(E4M3), scales=xs[m][:], in_=grp[:])
+
+        def quant_x(m):
+            nc.vector.quantize_mx(out=xc[m][:].bitcast(E4M3), scales=xs[m][:], in_=xg[m][:])
 
         bc = [[[keep.tile([P, NB], U32, name="bc%d%d%d" % (a, g, h), align_bytes=64) for h in range(2)] for g in range(4)] for a in range(2)]
         bs = [[[keep.tile([P, NB], U8, name="bs%d%d%d" % (a, g, h), align_bytes=64) for h in range(2)] for g in range(4)] for a in range(2)]
 
-        def do_back(k, on_scalar):
-            a, g, h = (0, k // 2, k % 2) if k < 8 else (1, k % 4, (k - 8) // 4)
-            grp = work.tile([P, NB, 4], BF16, name="bg", align_bytes=64, bufs=4)
-            dst = grp[:].rearrange("p (c i) t -> p c t i", i=4)
-            src = raw[a][g][:, :, h * NB : (h + 1) * NB].rearrange("p t (c i) -> p c t i", i=4)
+        bg = {}
+
+        def where(k):
+            return (0, k // 2, k % 2) if k < 8 else (1, k % 4, (k - 8) // 4)
+
+        def weave(k, on_scalar):
+            a, g, h = where(k)
+            bg[k] = work.tile([P, NB, 4], BF16, name="bg", align_bytes=64, bufs=4)
+            dst = bg[k][:].rearrange("p (c i) t -> p c t i", i=4)
+            src = raw[a, g, h][:] if (a, g) in SPLIT else raw[a, g, 0][:, :, h * NB : (h + 1) * NB]
+            src = src.rearrange("p t (c i) -> p c t i", i=4)
             if on_scalar:
                 nc.scalar.copy(out=dst, in_=src)
             else:
                 nc.vector.tensor_copy(out=dst, in_=src)
+
+        def quant_b(k):
+            a, g, h = where(k)
             nc.vector.quantize_mx(
-                out=bc[a][g][h][:].bitcast(E4M3), scales=bs[a][g][h][:], in_=grp[:].rearrange("p c t -> p (c t)")
+                out=bc[a][g][h][:].bitcast(E4M3), scales=bs[a][g][h][:], in_=bg[k][:].rearrange("p c t -> p (c t)")
             )
 
         banks = {}
@@ -133,45 +161,100 @@ def tile_fresnel_magnitude_residual_s9_kernel(
             for g in range(2):
                 for a in range(2):
                     col = g * F + c * NB
+                    w = [i for i, (lo, hi) in enumerate(FW) if lo <= c * NB < hi][0]
+                    at = 2 * (c * NB - FW[w][0])
                     nc.tensor.matmul_mx(
                         out=banks[u][a][:],
                         lhsT=xc[m][:, g * P : (g + 1) * P].bitcast(E4M3),
                         lhsT_scale=xs[m][:, g * P : (g + 1) * P],
-                        rhs=fwd[a][:, 2 * col : 2 * (col + NB)].bitcast(E2M1),
+                        rhs=fwd[a][w][:, g, at : at + 2 * NB].bitcast(E2M1),
                         rhs_scale=planes[:, a * 2 * F + col : a * 2 * F + col + NB],
                         start=(g == 0),
                         stop=(g == 1),
                     )
 
+        sq = {}
+        et = {}
         r2 = {}
+        mag = {}
         e_sb = {}
 
         def squares(u):
-            re, im = banks[u]
-            sr = work.tile([P, NB], F32, name="sr", align_bytes=64)
-            si = work.tile([P, NB], F32, name="si", align_bytes=64)
-            nc.scalar.activation(out=sr[:], in_=re[:], func=ACT.Square)
-            nc.scalar.activation(out=si[:], in_=im[:], func=ACT.Square)
-            r2[u] = work.tile([P, NB], F32, name="rr", align_bytes=64)
-            nc.vector.tensor_tensor(out=r2[u][:], in0=sr[:], in1=si[:], op=ALU.add)
+            sq[u] = [work.tile([P, NB], F32, name="sq%d" % a, align_bytes=64) for a in range(2)]
+            for a in range(2):
+                if u in T_UNITS:
+                    nc.scalar.activation(
+                        out=sq[u][a][:].rearrange("m (t p) -> m t p", t=4),
+                        in_=banks[u][a][:].rearrange("m (p t) -> m t p", t=4),
+                        func=ACT.Square,
+                    )
+                else:
+                    nc.scalar.activation(out=sq[u][a][:], in_=banks[u][a][:], func=ACT.Square)
 
-        def residual(u):
+        r2t = {}
+        tm = {}
+
+        def turn_add(u):
             m, c = divmod(u, 4)
-            mag = work.tile([P, NB], F32, name="mag", align_bytes=64)
-            nc.scalar.activation(out=mag[:], in_=r2[u][:], func=ACT.Sqrt)
+            r2t[u] = ps.tile([P, 4, P], F32, name="tp", tag="tp", bufs=1)
+            for t in range(4):
+                for a in range(2):
+                    nc.tensor.matmul(
+                        r2t[u][:, t, :],
+                        lhsT=sq[u][a][:, t * P : (t + 1) * P],
+                        rhs=ident[:],
+                        start=(a == 0),
+                        stop=(a == 1),
+                        is_transpose=True,
+                    )
+            mw = meas_sb[m][:].bitcast(F32)
+            tm[u] = ps.tile([P, 4, P], F32, name="acc", tag="acc", bufs=3)
+            for w in range(2):
+                nc.tensor.transpose(tm[u][:, w, :], mw[:, 256 * c + w : 256 * (c + 1) : 2], ident[:])
+
+        def root_t(u):
+            mag[u] = work.tile([P, P, 4], F32, name="mag", align_bytes=64)
+            nc.scalar.activation(out=mag[u][:], in_=r2t[u][:].rearrange("p t m -> p m t"), func=ACT.Sqrt)
+
+        def sub_t(u):
+            et[u, "t"] = work.tile([P, P, 4], BF16, name="ew", align_bytes=64, bufs=3)
+            nc.vector.tensor_tensor(
+                out=et[u, "t"][:].rearrange("p m (u e) -> p m u e", u=2),
+                in0=mag[u][:].rearrange("p m (u e) -> p m u e", u=2),
+                in1=tm[u][:].bitcast(BF16)[:, 0:2, :].rearrange("p u (m e) -> p m u e", e=2),
+                op=ALU.subtract,
+            )
+
+        def quant_t(u):
+            lo = (u % 2) * P
+            nc.vector.quantize_mx(
+                out=ec[u // 2][:, lo : lo + P].bitcast(E5M2),
+                scales=es[u // 2][:, lo : lo + P],
+                in_=et[u, "t"][:].rearrange("p m t -> p (m t)"),
+            )
+
+        def add(u):
+            r2[u] = work.tile([P, NB], F32, name="rr", align_bytes=64)
+            nc.vector.tensor_tensor(out=r2[u][:], in0=sq[u][0][:], in1=sq[u][1][:], op=ALU.add)
+
+        def root(u):
+            mag[u] = work.tile([P, NB], F32, name="mag", align_bytes=64)
+            nc.scalar.activation(out=mag[u][:], in_=r2[u][:], func=ACT.Sqrt)
+
+        def sub(u):
+            m, c = divmod(u, 4)
             if u % 2 == 0:
                 e_sb[u // 2] = work.tile([P, 2 * NB], BF16, name="e", align_bytes=64)
             lo = (u % 2) * NB
             nc.vector.tensor_tensor(
                 out=e_sb[u // 2][:, lo : lo + NB].rearrange("m (u p e) -> m u p e", u=2, e=2),
-                in0=mag[:].rearrange("m (p u e) -> m u p e", u=2, e=2),
+                in0=mag[u][:].rearrange("m (p u e) -> m u p e", u=2, e=2),
                 in1=meas_sb[m][:, c * NB : (c + 1) * NB].rearrange("m (p u e) -> m u p e", u=2, e=2),
                 op=ALU.subtract,
             )
 
         ec = [keep.tile([P, 256], U32, name="ec%d" % k, align_bytes=64) for k in range(8)]
         es = [keep.tile([P, 256], U8, name="es%d" % k, align_bytes=64) for k in range(8)]
-        et = {}
 
         def turn(k):
             ew = e_sb[k][:].bitcast(F32)
@@ -179,19 +262,33 @@ def tile_fresnel_magnitude_residual_s9_kernel(
             for q in range(4):
                 nc.tensor.transpose(et[k][:, q, :], ew[:, q * P : (q + 1) * P], ident[:])
 
-        def quant_e(k):
-            grp = work.tile([P, 1024], BF16, name="eg", align_bytes=64, bufs=2)
+        eg = {}
+
+        def copy_e(k):
+            eg[k] = work.tile([P, 1024], BF16, name="eg", align_bytes=64, bufs=2)
             nc.scalar.copy(
-                out=grp[:].bitcast(F32).rearrange("p (c r u) -> p c r u", c=2, u=2),
+                out=eg[k][:].bitcast(F32).rearrange("p (c r u) -> p c r u", c=2, u=2),
                 in_=et[k][:].rearrange("p (c u) r -> p c r u", u=2),
             )
-            nc.vector.quantize_mx(out=ec[k][:].bitcast(E5M2), scales=es[k][:], in_=grp[:])
+
+        def quant_e(k):
+            nc.vector.quantize_mx(out=ec[k][:].bitcast(E5M2), scales=es[k][:], in_=eg[k][:])
+
+        PRE = [(0, False), (1, False)]
+        V_AT = {8: [3, 13], 7: [5], 6: [6], 4: [7], 11: [8, 10], 9: [9], 14: [11], 17: [12], 16: [14]}
+        S_AT = {8: [2], 10: [4], 17: [15]}
+        XT = [0, 1, 8]
+        SV = 20
+        MC = 2
+        HALF = True
 
         acc = {}
+        ring = ("acc", "acc", "acc")
 
-        def cell(m, a, h):
-            acc[m, a, h] = ps.tile([P, NB], F32, name="acc", tag="acc", bufs=3)
-            for g in range(4):
+        def passes(m, a, h, gs, tag):
+            if gs[0] == 0:
+                acc[m, a, h] = ps.tile([P, NB], F32, name=tag, tag=tag, bufs=3 if tag == "acc" else 1 if tag == "tp" else 2)
+            for g in gs:
                 k, lo = 2 * m + g // 2, (g % 2) * P
                 nc.tensor.matmul_mx(
                     out=acc[m, a, h][:],
@@ -204,7 +301,7 @@ def tile_fresnel_magnitude_residual_s9_kernel(
                 )
 
         def store(m, a, h, on_scalar):
-            res = work.tile([P, NB], F32, name="res", align_bytes=64, bufs=4)
+            res = work.tile([P, NB], F32, name="res", align_bytes=64, bufs=6)
             if on_scalar:
                 nc.scalar.copy(out=res[:], in_=acc[m, a, h][:])
             else:
@@ -213,37 +310,79 @@ def tile_fresnel_magnitude_residual_s9_kernel(
 
         e_slot = {}
         b_slot = {}
-        pending = [(m, a, h) for a in range(2) for h in range(2) for m in range(4)]
+        pending = [(m, a, h) for m in range(4) for a in range(2) for h in range(2)]
+        half = {}
+        waiting = []
         n_out = 0
-        do_x(0)
+        turn_x(0)
+        quant_x(0)
+        for k, s in PRE:
+            weave(k, s)
         stage1(0)
+        for k, s in PRE:
+            quant_b(k)
+            b_slot[k] = -1
         stage1(1)
-        for u in range(24):
+        nt = 0
+        for u in range(26):
             if u < 16:
                 squares(u)
-            if u + 2 < 16:
-                stage1(u + 2)
-            if 1 <= u <= 16:
-                residual(u - 1)
-            if 2 <= u <= 16 and u % 2 == 0:
-                turn(u // 2 - 1)
-            if 3 <= u <= 17 and u % 2 == 1:
-                quant_e((u - 3) // 2)
-                e_slot[(u - 3) // 2] = u
-            if u in (1, 3, 5):
-                do_x((u + 1) // 2)
-            for k in range(16):
-                if (k * 3) // 4 == u:
-                    do_back(k, k in (1, 4, 7))
-                    b_slot[k] = u
-            ready = [
+            for m, a, h in waiting:
+                store(m, a, h, u < SV or n_out % 2 == 0)
+                n_out += 1
+            waiting = []
+            open_now = [c for c in half if half[c] == 2]
+            bready = [
                 (m, a, h)
                 for m, a, h in pending
-                if all(e_slot.get(2 * m + i, 99) < u for i in range(2))
-                and all(b_slot.get(k, 99) < u for k in ((h, 2 + h, 4 + h, 6 + h) if a == 0 else range(8 + 4 * h, 12 + 4 * h)))
+                if all(b_slot.get(k, 99) < u for k in ((h, 2 + h, 4 + h, 6 + h) if a == 0 else range(8 + 4 * h, 12 + 4 * h)))
             ]
-            for m, a, h in ready[:3]:
+            ready = [c for c in bready if all(e_slot.get(2 * c[0] + i, 99) < u for i in range(2))]
+            for m, a, h in ready[: MC if u < 16 else 4]:
                 pending.remove((m, a, h))
-                cell(m, a, h)
-                store(m, a, h, n_out % 2 == 0)
-                n_out += 1
+                if (m, a, h) in half:
+                    passes(m, a, h, range(2, 4), "")
+                else:
+                    passes(m, a, h, range(4), "acc" if u < 16 else ("re", "im", "acc")[nt % 3])
+                    nt += u >= 16
+                waiting.append((m, a, h))
+            if u >= 16 and HALF:
+                for m, a, h in [c for c in bready if c in pending and e_slot.get(2 * c[0], 99) < u and c not in half][: 4 - len(waiting)]:
+                    half[m, a, h] = 2
+                    passes(m, a, h, range(2), ("re", "im", "acc")[nt % 3])
+                    nt += 1
+            if u in T_UNITS:
+                turn_add(u)
+            if u + 2 < 16:
+                stage1(u + 2)
+            if 2 <= u < 18:
+                (sub_t if u - 2 in T_UNITS else sub)(u - 2)
+            for k in V_AT.get(u, ()):
+                weave(k, False)
+            if u < 16 and u not in T_UNITS:
+                add(u)
+            if u - 2 in T_UNITS:
+                quant_t(u - 2)
+                e_slot[(u - 2) // 2] = u if u % 2 else 99
+            if 1 <= u <= 16:
+                (root_t if u - 1 in T_UNITS else root)(u - 1)
+            for k in S_AT.get(u - 1, ()):
+                quant_b(k)
+                b_slot[k] = u
+            for k in V_AT.get(u, ()):
+                quant_b(k)
+                b_slot[k] = u
+            if 3 <= u <= 17 and u % 2 == 1 and u - 3 not in T_UNITS:
+                turn((u - 3) // 2)
+            if 4 <= u <= 18 and u % 2 == 0 and u - 4 not in T_UNITS:
+                copy_e(u // 2 - 2)
+                quant_e(u // 2 - 2)
+                e_slot[u // 2 - 2] = u
+            for k in S_AT.get(u, ()):
+                weave(k, True)
+            if u in XT:
+                turn_x(XT.index(u) + 1)
+            if u - 1 in XT:
+                quant_x(XT.index(u - 1) + 1)
+            if u > 19 and not pending and not waiting:
+                break

@@ -18,7 +18,7 @@ ACT = mybir.ActivationFunctionType
 ALU = mybir.AluOpType
 
 P = 128
-T_UNITS = (4, 5, 6, 7, 8, 9, 10, 11)
+T_UNITS = ()
 FW = ((0, 512), (512, 1024), (1024, 2048))
 SPLIT = ((0, 0),)
 NB = 512
@@ -83,28 +83,28 @@ def tile_fresnel_magnitude_residual_s9_kernel(
                 src = src[:, :, h * NB : (h + 1) * NB]
             nc.sync.dma_start(out=raw[a, g, h][:], in_=src)
 
-        load_x(0)
         load_fwd(0)
-        load_back(0, 0, 1)
+        load_x(0)
         load_scales(1, nc.sync)
-        load_back(0, 0, 0)
+        load_back(0, 0, 1)
         load_fwd(1)
         load_scales(0, nc.sync)
+        load_back(0, 0, 0)
         load_fwd(2)
         load_x(1)
-        load_meas(1)
-        load_x(2)
-        load_meas(0)
-        load_back(0, 3)
-        load_back(1, 1)
         load_x(3)
-        load_meas(2)
-        load_back(0, 2)
-        load_back(1, 2)
+        load_meas(0)
         load_back(0, 1)
-        load_meas(3)
-        load_back(1, 0)
         load_back(1, 3)
+        load_x(2)
+        load_meas(1)
+        load_back(0, 2)
+        load_back(0, 3)
+        load_meas(2)
+        load_back(1, 2)
+        load_back(1, 0)
+        load_back(1, 1)
+        load_meas(3)
 
         xc = [keep.tile([P, 256], U32, name="xc%d" % m, align_bytes=64) for m in range(4)]
         xs = [keep.tile([P, 256], U8, name="xs%d" % m, align_bytes=64) for m in range(4)]
@@ -158,8 +158,8 @@ def tile_fresnel_magnitude_residual_s9_kernel(
             re = ps.tile([P, NB], F32, name="re", tag="re", bufs=2)
             im = ps.tile([P, NB], F32, name="im", tag="im", bufs=2)
             banks[u] = (re, im)
-            for g in range(2):
-                for a in range(2):
+            for a in range(2):
+                for g in range(2):
                     col = g * F + c * NB
                     w = [i for i, (lo, hi) in enumerate(FW) if lo <= c * NB < hi][0]
                     at = 2 * (c * NB - FW[w][0])
@@ -247,9 +247,9 @@ def tile_fresnel_magnitude_residual_s9_kernel(
                 e_sb[u // 2] = work.tile([P, 2 * NB], BF16, name="e", align_bytes=64)
             lo = (u % 2) * NB
             nc.vector.tensor_tensor(
-                out=e_sb[u // 2][:, lo : lo + NB].rearrange("m (u p e) -> m u p e", u=2, e=2),
-                in0=mag[u][:].rearrange("m (p u e) -> m u p e", u=2, e=2),
-                in1=meas_sb[m][:, c * NB : (c + 1) * NB].rearrange("m (p u e) -> m u p e", u=2, e=2),
+                out=e_sb[u // 2][:, lo : lo + NB],
+                in0=mag[u][:],
+                in1=meas_sb[m][:, c * NB : (c + 1) * NB],
                 op=ALU.subtract,
             )
 
@@ -260,7 +260,8 @@ def tile_fresnel_magnitude_residual_s9_kernel(
             ew = e_sb[k][:].bitcast(F32)
             et[k] = ps.tile([P, 4, P], F32, name="tp", tag="tp", bufs=1)
             for q in range(4):
-                nc.tensor.transpose(et[k][:, q, :], ew[:, q * P : (q + 1) * P], ident[:])
+                c, w = divmod(q, 2)
+                nc.tensor.transpose(et[k][:, q, :], ew[:, 256 * c + w : 256 * (c + 1) : 2], ident[:])
 
         eg = {}
 
@@ -274,12 +275,12 @@ def tile_fresnel_magnitude_residual_s9_kernel(
         def quant_e(k):
             nc.vector.quantize_mx(out=ec[k][:].bitcast(E5M2), scales=es[k][:], in_=eg[k][:])
 
-        PRE = [(0, False), (1, False)]
-        V_AT = {8: [3, 13], 7: [5], 6: [6], 4: [7], 11: [8, 10], 9: [9], 14: [11], 17: [12], 16: [14]}
-        S_AT = {8: [2], 10: [4], 17: [15]}
-        XT = [0, 1, 8]
+        PRE = [(0, False), (1, True)]
+        V_AT = {4: [2], 12: [3], 7: [4], 14: [5, 6], 16: [8, 11], 18: [13, 14], 19: [15]}
+        S_AT = {14: [7], 16: [9], 15: [10], 18: [12]}
+        XT = [0, 4, 8]
         SV = 20
-        MC = 2
+        MC = 1
         HALF = True
 
         acc = {}

@@ -38,15 +38,15 @@ def tile_fresnel_magnitude_residual_s9_kernel(
         work = ctx.enter_context(tc.tile_pool(name="work", bufs=3))
         ps = ctx.enter_context(tc.psum_pool(name="ps", bufs=2))
 
+        warm = keep.tile([P, 1], F32, name="warm")
+        nc.gpsimd.memset(warm[:], 1.0)
+        nc.scalar.activation(out=warm[:], in_=warm[:], func=ACT.Sqrt)
         ident = keep.tile([P, P], F32, name="ident", align_bytes=64)
         make_identity(nc, ident[:])
-        warm = keep.tile([P, 1], F32, name="warm")
-        nc.vector.memset(warm[:], 1.0)
-        nc.scalar.activation(out=warm[:], in_=warm[:], func=ACT.Sqrt)
-        planes = keep.tile([P, 2 * 2 * F], U8, name="planes", align_bytes=64)
-        nc.vector.memset(planes[:].bitcast(I32), 0)
+        planes = [keep.tile([P, 2 * F], U8, name="planes%d" % a, align_bytes=64) for a in range(2)]
+        for a in range(2):
+            nc.vector.memset(planes[a][:].bitcast(I32), 0)
 
-        ctx.enter_context(tc.manual_schedule())
         x_sb = [keep.tile([P, K], BF16, name="x%d" % m, align_bytes=64) for m in range(4)]
         meas_sb = [keep.tile([P, F], BF16, name="meas%d" % m, align_bytes=64) for m in range(4)]
         fwd = [{c: keep.tile([P, 2, 2 * (hi - lo)], U8, name="fwd%d%d" % (a, c), align_bytes=64) for c, (lo, hi) in enumerate(FW)} for a in range(2)]
@@ -65,7 +65,7 @@ def tile_fresnel_magnitude_residual_s9_kernel(
         def load_scales(a, queue):
             if True:
                 for r in range(4):
-                    dst = planes[r:P:32, a * 2 * F : (a + 1) * 2 * F].bitcast(I32)
+                    dst = planes[a][r:P:32, :].bitcast(I32)
                     src = scales[a][:, r:16:4, :].bitcast(I32)
                     queue.dma_start(out=dst.rearrange("q (g n) -> q g n", g=2), in_=src.rearrange("g q n -> q g n"))
 
@@ -83,42 +83,47 @@ def tile_fresnel_magnitude_residual_s9_kernel(
                 src = src[:, :, h * NB : (h + 1) * NB]
             nc.sync.dma_start(out=raw[a, g, h][:], in_=src)
 
-        load_fwd(0)
         load_x(0)
+        load_fwd(0)
+        load_scales(0, nc.sync)
         load_scales(1, nc.sync)
         load_back(0, 0, 1)
         load_fwd(1)
-        load_scales(0, nc.sync)
         load_back(0, 0, 0)
         load_fwd(2)
-        load_x(1)
-        load_x(3)
         load_meas(0)
+        load_x(1)
         load_back(0, 1)
-        load_back(1, 3)
-        load_x(2)
         load_meas(1)
+        load_x(2)
         load_back(0, 2)
         load_back(0, 3)
         load_meas(2)
-        load_back(1, 2)
+        load_x(3)
         load_back(1, 0)
         load_back(1, 1)
         load_meas(3)
+        load_back(1, 2)
+        load_back(1, 3)
 
         xc = [keep.tile([P, 256], U32, name="xc%d" % m, align_bytes=64) for m in range(4)]
         xs = [keep.tile([P, 256], U8, name="xs%d" % m, align_bytes=64) for m in range(4)]
 
         xg = {}
+        xt = {}
 
         def turn_x(m):
             xw = x_sb[m][:].bitcast(F32)
-            bank = ps.tile([P, 4, P], F32, name="tp", tag="tp", bufs=1)
+            bank = ps.tile([P, 4, P], F32, name="xt", tag="acc", bufs=3)
             for g in range(2):
                 for u in range(2):
                     nc.tensor.transpose(bank[:, 2 * g + u, :], xw[:, 256 * g + u : 256 * (g + 1) : 2], ident[:])
-            xg[m] = work.tile([P, 1024], BF16, name="xg", align_bytes=64, bufs=2)
-            nc.vector.tensor_copy(
+            xt[m] = bank
+
+        def copy_x(m):
+            bank = xt[m]
+            xg[m] = work.tile([P, 1024], BF16, name="xg", align_bytes=64, bufs=3)
+            nc.scalar.copy(
                 out=xg[m][:].bitcast(F32).rearrange("p (g r u) -> p g r u", g=2, u=2),
                 in_=bank[:].rearrange("p (g u) r -> p g r u", u=2),
             )
@@ -168,7 +173,7 @@ def tile_fresnel_magnitude_residual_s9_kernel(
                         lhsT=xc[m][:, g * P : (g + 1) * P].bitcast(E4M3),
                         lhsT_scale=xs[m][:, g * P : (g + 1) * P],
                         rhs=fwd[a][w][:, g, at : at + 2 * NB].bitcast(E2M1),
-                        rhs_scale=planes[:, a * 2 * F + col : a * 2 * F + col + NB],
+                        rhs_scale=planes[a][:, col : col + NB],
                         start=(g == 0),
                         stop=(g == 1),
                     )
@@ -275,13 +280,13 @@ def tile_fresnel_magnitude_residual_s9_kernel(
         def quant_e(k):
             nc.vector.quantize_mx(out=ec[k][:].bitcast(E5M2), scales=es[k][:], in_=eg[k][:])
 
-        PRE = [(0, False), (1, True)]
-        V_AT = {4: [2], 12: [3], 7: [4], 14: [5, 6], 16: [8, 11], 18: [13, 14], 19: [15]}
-        S_AT = {14: [7], 16: [9], 15: [10], 18: [12]}
-        XT = [0, 4, 8]
-        SV = 20
-        MC = 1
-        HALF = True
+        PRE = []
+        V_AT = {0: [0, 1], 2: [2], 3: [3], 5: [4], 6: [5], 7: [6], 8: [7], 10: [8], 11: [9], 12: [10], 14: [12], 16: [14]}
+        S_AT = {13: [11], 15: [13], 16: [15]}
+        XT = [1, 5, 9]
+        SV = 16
+        MC = 2
+        HALF = False
 
         acc = {}
         ring = ("acc", "acc", "acc")
@@ -301,8 +306,9 @@ def tile_fresnel_magnitude_residual_s9_kernel(
                     stop=(g == 3),
                 )
 
-        def store(m, a, h, on_scalar):
-            res = work.tile([P, NB], F32, name="res", align_bytes=64, bufs=6)
+        def store(m, a, h, on_scalar, u, n_out):
+            tag = "res" if u < 17 else ("sq0", "sq1", "rr", "mag")[n_out % 4]
+            res = work.tile([P, NB], F32, name=tag, tag=tag, align_bytes=64, bufs=3)
             if on_scalar:
                 nc.scalar.copy(out=res[:], in_=acc[m, a, h][:])
             else:
@@ -316,6 +322,7 @@ def tile_fresnel_magnitude_residual_s9_kernel(
         waiting = []
         n_out = 0
         turn_x(0)
+        copy_x(0)
         quant_x(0)
         for k, s in PRE:
             weave(k, s)
@@ -329,7 +336,7 @@ def tile_fresnel_magnitude_residual_s9_kernel(
             if u < 16:
                 squares(u)
             for m, a, h in waiting:
-                store(m, a, h, u < SV or n_out % 2 == 0)
+                store(m, a, h, u < SV or n_out % 3 != 1, u, n_out)
                 n_out += 1
             waiting = []
             open_now = [c for c in half if half[c] == 2]
@@ -348,12 +355,15 @@ def tile_fresnel_magnitude_residual_s9_kernel(
                     nt += u >= 16
                 waiting.append((m, a, h))
             if u >= 16 and HALF:
-                for m, a, h in [c for c in bready if c in pending and e_slot.get(2 * c[0], 99) < u and c not in half][: 4 - len(waiting)]:
+                for m, a, h in [c for c in bready if c in pending and e_slot.get(2 * c[0], 99) < u and c not in half][: 4 - nt]:
                     half[m, a, h] = 2
-                    passes(m, a, h, range(2), ("re", "im", "acc")[nt % 3])
+                    passes(m, a, h, range(2), ("re", "im")[nt % 2])
                     nt += 1
             if u in T_UNITS:
                 turn_add(u)
+            for m in range(1, 4):
+                if XT[m - 1] == u - 1:
+                    quant_x(m)
             if u + 2 < 16:
                 stage1(u + 2)
             if 2 <= u < 18:
@@ -381,9 +391,11 @@ def tile_fresnel_magnitude_residual_s9_kernel(
                 e_slot[u // 2 - 2] = u
             for k in S_AT.get(u, ()):
                 weave(k, True)
-            if u in XT:
-                turn_x(XT.index(u) + 1)
-            if u - 1 in XT:
-                quant_x(XT.index(u - 1) + 1)
+            for m in range(1, 4):
+                if XT[m - 1] == u:
+                    turn_x(m)
+            for m in range(1, 4):
+                if XT[m - 1] == u:
+                    copy_x(m)
             if u > 19 and not pending and not waiting:
                 break

@@ -320,6 +320,7 @@ def tile_fresnel_magnitude_residual_s9_kernel(
         pending = [(m, a, h) for m in range(4) for a in range(2) for h in range(2)]
         half = {}
         waiting = []
+        lag = []
         n_out = 0
         turn_x(0)
         copy_x(0)
@@ -381,8 +382,13 @@ def tile_fresnel_magnitude_residual_s9_kernel(
                 quant_b(k)
                 b_slot[k] = u
             for k in V_AT.get(u, ()):
-                quant_b(k)
-                b_slot[k] = u
+                lag.append(k)
+                if len(lag) > 1:
+                    quant_b(lag[0])
+                    b_slot[lag.pop(0)] = u
+            if lag and not any(V_AT.get(v) for v in range(u + 1, 26)):
+                quant_b(lag[0])
+                b_slot[lag.pop(0)] = u
             if 3 <= u <= 17 and u % 2 == 1 and u - 3 not in T_UNITS:
                 turn((u - 3) // 2)
             if 4 <= u <= 18 and u % 2 == 0 and u - 4 not in T_UNITS:

from contextlib import ExitStack

import concourse.mybir as mybir
from concourse.masks import make_identity

M, K, F, N = 512, 1024, 2048, 1024
FLOPS = 2 * M * K * F * 2 + 2 * M * F * N * 2

F32 = mybir.dt.float32
BF16 = mybir.dt.bfloat16
I32 = mybir.dt.int32
U32 = mybir.dt.uint32
U8 = mybir.dt.uint8
E4M3 = mybir.dt.float8_e4m3fn_x4
E5M2 = mybir.dt.float8_e5m2_x4
E2M1 = mybir.dt.float4_e2m1fn_x4
ACT = mybir.ActivationFunctionType
ALU = mybir.AluOpType

P = 128
T_UNITS = ()
FW = ((0, 512), (512, 1024), (1024, 2048))
SPLIT = ((0, 0),)
NB = 512


def tile_fresnel_magnitude_residual_s9_kernel(
    tc, x, cos_words, cos_scales, sin_words, sin_scales, meas, back_cos, back_sin, out_re, out_im
):
    nc = tc.nc
    words = (cos_words, sin_words)
    scales = (cos_scales, sin_scales)
    back = (back_cos, back_sin)
    outs = (out_re, out_im)

    with ExitStack() as ctx:
        keep = ctx.enter_context(tc.tile_pool(name="keep", bufs=1))
        work = ctx.enter_context(tc.tile_pool(name="work", bufs=3))
        ps = ctx.enter_context(tc.psum_pool(name="ps", bufs=2))

        warm = keep.tile([P, 1], F32, name="warm")
        nc.gpsimd.memset(warm[:], 1.0)
        nc.scalar.activation(out=warm[:], in_=warm[:], func=ACT.Sqrt)
        ident = keep.tile([P, P], F32, name="ident", align_bytes=64)
        make_identity(nc, ident[:])
        planes = [keep.tile([P, 2 * F], U8, name="planes%d" % a, align_bytes=64) for a in range(2)]
        for a in range(2):
            nc.vector.memset(planes[a][:].bitcast(I32), 0)

        x_sb = [keep.tile([P, K], BF16, name="x%d" % m, align_bytes=64) for m in range(4)]
        meas_sb = [keep.tile([P, F], BF16, name="meas%d" % m, align_bytes=64) for m in range(4)]
        fwd = [{c: keep.tile([P, 2, 2 * (hi - lo)], U8, name="fwd%d%d" % (a, c), align_bytes=64) for c, (lo, hi) in enumerate(FW)} for a in range(2)]
        raw = {}
        for a in range(2):
            for g in range(4):
                for h in range(2 if (a, g) in SPLIT else 1):
                    raw[a, g, h] = keep.tile([P, 4, NB if (a, g) in SPLIT else N], BF16, name="raw%d%d%d" % (a, g, h), align_bytes=64)

        def load_x(m):
            nc.sync.dma_start(out=x_sb[m][:], in_=x[m * P : (m + 1) * P, :])

        def load_meas(m):
            nc.sync.dma_start(out=meas_sb[m][:], in_=meas[m * P : (m + 1) * P, :])

        def load_scales(a, queue):
            if True:
                for r in range(4):
                    dst = planes[a][r:P:32, :].bitcast(I32)
                    src = scales[a][:, r:16:4, :].bitcast(I32)
                    queue.dma_start(out=dst.rearrange("q (g n) -> q g n", g=2), in_=src.rearrange("g q n -> q g n"))

        def load_fwd(c):
            lo, hi = FW[c]
            for a in range(2):
                nc.sync.dma_start(
                    out=fwd[a][c][:].bitcast(I32),
                    in_=words[a].bitcast(I32)[:, :, lo // 2 : hi // 2].rearrange("g p w -> p g w"),
                )

        def load_back(a, g, h=0):
            src = back[a][g * 512 : (g + 1) * 512, :].rearrange("(p j) w -> p j w", j=4)
            if (a, g) in SPLIT:
                src = src[:, :, h * NB : (h + 1) * NB]
            nc.sync.dma_start(out=raw[a, g, h][:], in_=src)

        load_x(0)
        load_fwd(0)
        load_scales(0, nc.sync)
        load_scales(1, nc.sync)
        load_back(0, 0, 1)
        load_fwd(1)
        load_back(0, 0, 0)
        load_fwd(2)
        load_meas(0)
        load_x(1)
        load_back(0, 1)
        load_meas(1)
        load_x(2)
        load_back(0, 2)
        load_back(0, 3)
        load_meas(2)
        load_x(3)
        load_back(1, 0)
        load_back(1, 1)
        load_meas(3)
        load_back(1, 2)
        load_back(1, 3)

        xc = [keep.tile([P, 256], U32, name="xc%d" % m, align_bytes=64) for m in range(4)]
        xs = [keep.tile([P, 256], U8, name="xs%d" % m, align_bytes=64) for m in range(4)]

        xg = {}
        xt = {}

        def turn_x(m):
            xw = x_sb[m][:].bitcast(F32)
            bank = ps.tile([P, 4, P], F32, name="xt", tag="acc", bufs=3)
            for g in range(2):
                for u in range(2):
                    nc.tensor.transpose(bank[:, 2 * g + u, :], xw[:, 256 * g + u : 256 * (g + 1) : 2], ident[:])
            xt[m] = bank

        def copy_x(m):
            bank = xt[m]
            xg[m] = work.tile([P, 1024], BF16, name="xg", align_bytes=64, bufs=3)
            nc.scalar.copy(
                out=xg[m][:].bitcast(F32).rearrange("p (g r u) -> p g r u", g=2, u=2),
                in_=bank[:].rearrange("p (g u) r -> p g r u", u=2),
            )

        def quant_x(m):
            nc.vector.quantize_mx(out=xc[m][:].bitcast(E4M3), scales=xs[m][:], in_=xg[m][:])

        bc = [[[keep.tile([P, NB], U32, name="bc%d%d%d" % (a, g, h), align_bytes=64) for h in range(2)] for g in range(4)] for a in range(2)]
        bs = [[[keep.tile([P, NB], U8, name="bs%d%d%d" % (a, g, h), align_bytes=64) for h in range(2)] for g in range(4)] for a in range(2)]

        bg = {}

        def where(k):
            return (0, k // 2, k % 2) if k < 8 else (1, k % 4, (k - 8) // 4)

        def weave(k, on_scalar):
            a, g, h = where(k)
            bg[k] = work.tile([P, NB, 4], BF16, name="bg", align_bytes=64, bufs=4)
            dst = bg[k][:].rearrange("p (c i) t -> p c t i", i=4)
            src = raw[a, g, h][:] if (a, g) in SPLIT else raw[a, g, 0][:, :, h * NB : (h + 1) * NB]
            src = src.rearrange("p t (c i) -> p c t i", i=4)
            if on_scalar:
                nc.scalar.copy(out=dst, in_=src)
            else:
                nc.vector.tensor_copy(out=dst, in_=src)

        def quant_b(k):
            a, g, h = where(k)
            nc.vector.quantize_mx(
                out=bc[a][g][h][:].bitcast(E4M3), scales=bs[a][g][h][:], in_=bg[k][:].rearrange("p c t -> p (c t)")
            )

        banks = {}

        def stage1(u):
            m, c = divmod(u, 4)
            re = ps.tile([P, NB], F32, name="re", tag="re", bufs=2)
            im = ps.tile([P, NB], F32, name="im", tag="im", bufs=2)
            banks[u] = (re, im)
            for a in range(2):
                for g in range(2):
                    col = g * F + c * NB
                    w = [i for i, (lo, hi) in enumerate(FW) if lo <= c * NB < hi][0]
                    at = 2 * (c * NB - FW[w][0])
                    nc.tensor.matmul_mx(
                        out=banks[u][a][:],
                        lhsT=xc[m][:, g * P : (g + 1) * P].bitcast(E4M3),
                        lhsT_scale=xs[m][:, g * P : (g + 1) * P],
                        rhs=fwd[a][w][:, g, at : at + 2 * NB].bitcast(E2M1),
                        rhs_scale=planes[a][:, col : col + NB],
                        start=(g == 0),
                        stop=(g == 1),
                    )

        sq = {}
        et = {}
        r2 = {}
        mag = {}
        e_sb = {}

        def squares(u):
            sq[u] = [work.tile([P, NB], F32, name="sq%d" % a, align_bytes=64) for a in range(2)]
            for a in range(2):
                if u in T_UNITS:
                    nc.scalar.activation(
                        out=sq[u][a][:].rearrange("m (t p) -> m t p", t=4),
                        in_=banks[u][a][:].rearrange("m (p t) -> m t p", t=4),
                        func=ACT.Square,
                    )
                else:
                    nc.scalar.activation(out=sq[u][a][:], in_=banks[u][a][:], func=ACT.Square)

        r2t = {}
        tm = {}

        def turn_add(u):
            m, c = divmod(u, 4)
            r2t[u] = ps.tile([P, 4, P], F32, name="tp", tag="tp", bufs=1)
            for t in range(4):
                for a in range(2):
                    nc.tensor.matmul(
                        r2t[u][:, t, :],
                        lhsT=sq[u][a][:, t * P : (t + 1) * P],
                        rhs=ident[:],
                        start=(a == 0),
                        stop=(a == 1),
                        is_transpose=True,
                    )
            mw = meas_sb[m][:].bitcast(F32)
            tm[u] = ps.tile([P, 4, P], F32, name="acc", tag="acc", bufs=3)
            for w in range(2):
                nc.tensor.transpose(tm[u][:, w, :], mw[:, 256 * c + w : 256 * (c + 1) : 2], ident[:])

        def root_t(u):
            mag[u] = work.tile([P, P, 4], F32, name="mag", align_bytes=64)
            nc.scalar.activation(out=mag[u][:], in_=r2t[u][:].rearrange("p t m -> p m t"), func=ACT.Sqrt)

        def sub_t(u):
            et[u, "t"] = work.tile([P, P, 4], BF16, name="ew", align_bytes=64, bufs=3)
            nc.vector.tensor_tensor(
                out=et[u, "t"][:].rearrange("p m (u e) -> p m u e", u=2),
                in0=mag[u][:].rearrange("p m (u e) -> p m u e", u=2),
                in1=tm[u][:].bitcast(BF16)[:, 0:2, :].rearrange("p u (m e) -> p m u e", e=2),
                op=ALU.subtract,
            )

        def quant_t(u):
            lo = (u % 2) * P
            nc.vector.quantize_mx(
                out=ec[u // 2][:, lo : lo + P].bitcast(E5M2),
                scales=es[u // 2][:, lo : lo + P],
                in_=et[u, "t"][:].rearrange("p m t -> p (m t)"),
            )

        def add(u):
            r2[u] = work.tile([P, NB], F32, name="rr", align_bytes=64)
            nc.vector.tensor_tensor(out=r2[u][:], in0=sq[u][0][:], in1=sq[u][1][:], op=ALU.add)

        def root(u):
            mag[u] = work.tile([P, NB], F32, name="mag", align_bytes=64)
            nc.scalar.activation(out=mag[u][:], in_=r2[u][:], func=ACT.Sqrt)

        def sub(u):
            m, c = divmod(u, 4)
            if u % 2 == 0:
                e_sb[u // 2] = work.tile([P, 2 * NB], BF16, name="e", align_bytes=64)
            lo = (u % 2) * NB
            nc.vector.tensor_tensor(
                out=e_sb[u // 2][:, lo : lo + NB],
                in0=mag[u][:],
                in1=meas_sb[m][:, c * NB : (c + 1) * NB],
                op=ALU.subtract,
            )

        ec = [keep.tile([P, 256], U32, name="ec%d" % k, align_bytes=64) for k in range(8)]
        es = [keep.tile([P, 256], U8, name="es%d" % k, align_bytes=64) for k in range(8)]

        def turn(k):
            ew = e_sb[k][:].bitcast(F32)
            et[k] = ps.tile([P, 4, P], F32, name="tp", tag="tp", bufs=1)
            for q in range(4):
                c, w = divmod(q, 2)
                nc.tensor.transpose(et[k][:, q, :], ew[:, 256 * c + w : 256 * (c + 1) : 2], ident[:])

        eg = {}

        def copy_e(k):
            eg[k] = work.tile([P, 1024], BF16, name="eg", align_bytes=64, bufs=2)
            nc.scalar.copy(
                out=eg[k][:].bitcast(F32).rearrange("p (c r u) -> p c r u", c=2, u=2),
                in_=et[k][:].rearrange("p (c u) r -> p c r u", u=2),
            )

        def quant_e(k):
            nc.vector.quantize_mx(out=ec[k][:].bitcast(E5M2), scales=es[k][:], in_=eg[k][:])

        PRE = []
        V_AT = {0: [0, 1], 2: [2], 3: [3], 5: [4], 6: [5], 7: [6], 8: [7], 10: [8], 11: [9], 12: [10], 14: [12], 16: [14]}
        S_AT = {13: [11], 15: [13], 16: [15]}
        XT = [1, 5, 9]
        SV = 16
        MC = 2
        HALF = False

        acc = {}
        ring = ("acc", "acc", "acc")

        def passes(m, a, h, gs, tag):
            if gs[0] == 0:
                acc[m, a, h] = ps.tile([P, NB], F32, name=tag, tag=tag, bufs=3 if tag == "acc" else 1 if tag == "tp" else 2)
            for g in gs:
                k, lo = 2 * m + g // 2, (g % 2) * P
                nc.tensor.matmul_mx(
                    out=acc[m, a, h][:],
                    lhsT=ec[k][:, lo : lo + P].bitcast(E5M2),
                    lhsT_scale=es[k][:, lo : lo + P],
                    rhs=bc[a][g][h][:].bitcast(E4M3),
                    rhs_scale=bs[a][g][h][:],
                    start=(g == 0),
                    stop=(g == 3),
                )

        def store(m, a, h, on_scalar, u, n_out):
            tag = "res" if u < 17 else ("sq0", "sq1", "rr", "mag")[n_out % 4]
            res = work.tile([P, NB], F32, name=tag, tag=tag, align_bytes=64, bufs=3)
            if on_scalar:
                nc.scalar.copy(out=res[:], in_=acc[m, a, h][:])
            else:
                nc.vector.tensor_copy(out=res[:], in_=acc[m, a, h][:])
            nc.sync.dma_start(out=outs[a][m * P : (m + 1) * P, h * NB : (h + 1) * NB], in_=res[:])

        e_slot = {}
        b_slot = {}
        pending = [(m, a, h) for m in range(4) for a in range(2) for h in range(2)]
        half = {}
        waiting = []
        lag = []
        n_out = 0
        turn_x(0)
        copy_x(0)
        quant_x(0)
        for k, s in PRE:
            weave(k, s)
        stage1(0)
        for k, s in PRE:
            quant_b(k)
            b_slot[k] = -1
        stage1(1)
        nt = 0
        for u in range(26):
            if u < 16:
                squares(u)
            for m, a, h in waiting:
                store(m, a, h, u < SV or n_out % 3 != 1, u, n_out)
                n_out += 1
            waiting = []
            open_now = [c for c in half if half[c] == 2]
            bready = [
                (m, a, h)
                for m, a, h in pending
                if all(b_slot.get(k, 99) < u for k in ((h, 2 + h, 4 + h, 6 + h) if a == 0 else range(8 + 4 * h, 12 + 4 * h)))
            ]
            ready = [c for c in bready if all(e_slot.get(2 * c[0] + i, 99) < u for i in range(2))]
            for m, a, h in ready[: MC if u < 16 else 4]:
                pending.remove((m, a, h))
                if (m, a, h) in half:
                    passes(m, a, h, range(2, 4), "")
                else:
                    passes(m, a, h, range(4), "acc" if u < 16 else ("re", "im", "acc")[nt % 3])
                    nt += u >= 16
                waiting.append((m, a, h))
            if u >= 16 and HALF:
                for m, a, h in [c for c in bready if c in pending and e_slot.get(2 * c[0], 99) < u and c not in half][: 4 - nt]:
                    half[m, a, h] = 2
                    passes(m, a, h, range(2), ("re", "im")[nt % 2])
                    nt += 1
            if u in T_UNITS:
                turn_add(u)
            for m in range(1, 4):
                if XT[m - 1] == u - 1:
                    quant_x(m)
            if u + 2 < 16:
                stage1(u + 2)
            if 2 <= u < 18:
                (sub_t if u - 2 in T_UNITS else sub)(u - 2)
            for k in V_AT.get(u, ()):
                weave(k, False)
            if u < 16 and u not in T_UNITS:
                add(u)
            if u - 2 in T_UNITS:
                quant_t(u - 2)
                e_slot[(u - 2) // 2] = u if u % 2 else 99
            if 1 <= u <= 16:
                (root_t if u - 1 in T_UNITS else root)(u - 1)
            for k in S_AT.get(u - 1, ()):
                quant_b(k)
                b_slot[k] = u
            for k in V_AT.get(u, ()):
                lag.append(k)
                if len(lag) > 1:
                    quant_b(lag[0])
                    b_slot[lag.pop(0)] = u
            if lag and not any(V_AT.get(v) for v in range(u + 1, 26)):
                quant_b(lag[0])
                b_slot[lag.pop(0)] = u
            if 3 <= u <= 17 and u % 2 == 1 and u - 3 not in T_UNITS:
                turn((u - 3) // 2)
            if 4 <= u <= 18 and u % 2 == 0 and u - 4 not in T_UNITS:
                copy_e(u // 2 - 2)
                quant_e(u // 2 - 2)
                e_slot[u // 2 - 2] = u
            for k in S_AT.get(u, ()):
                weave(k, True)
            for m in range(1, 4):
                if XT[m - 1] == u:
                    turn_x(m)
            for m in range(1, 4):
                if XT[m - 1] == u:
                    copy_x(m)
            if u > 19 and not pending and not waiting:
                break
